import numpy as np
import ml_dtypes


def mxq(x, axis, fmt="e4m3"):
    dtype, down = {"e4m3": (ml_dtypes.float8_e4m3fn, 7), "e5m2": (ml_dtypes.float8_e5m2, 14)}[fmt]
    v = np.moveaxis(np.asarray(x, np.float32).astype(ml_dtypes.bfloat16).astype(np.float64), axis, -1)
    blocks = v.reshape(v.shape[:-1] + (-1, 32))
    amax = np.abs(blocks).max(-1, keepdims=True)
    byte = np.maximum(np.where(amax > 0, np.frexp(amax)[1] - 1 + 127, 0) - down, 1)
    scale = np.exp2(byte - 127.0)
    codes = (blocks / scale).astype(np.float32).astype(dtype).astype(np.float64)
    return np.moveaxis((codes * scale).reshape(v.shape), -1, axis)


WIDE = False


def mx_kscale(k):
    if not WIDE:
        return np.ones(k)
    levels = np.array([10, -10, 5, -5, 0])
    if k % 512:
        return np.exp2(np.random.permutation(np.resize(levels, k // 32))).repeat(32)
    a = np.empty((k // 512, 16))
    for p in range(k // 512):
        a[p, :8] = np.random.permutation(np.resize(levels, 8))
        for g in range(8):
            far = levels[np.abs(levels - a[p, g]) >= 10]
            a[p, g + 8] = far[np.random.randint(len(far))]
    return np.exp2(a.ravel()).repeat(32)


def f64(x):
    return np.asarray(x).astype(np.float64)


def striped(idx):
    return np.tile(idx.reshape(-1, 16).T, (8, 1)).astype(np.uint16)


def unstriped(offs):
    return offs[:16].T.reshape(-1).astype(np.int64)


def pack_weight(w):
    k, n = w.shape
    w = f64(np.asarray(w, np.float32).astype(ml_dtypes.bfloat16)).reshape(k // 32, 32, n)
    amax = np.abs(w).max(1)
    byte = np.clip(np.where(amax > 0, np.frexp(amax)[1] - 1 + 127 - 7, 1), 1, 254)
    scaled = (w * np.exp2(127.0 - byte)[:, None, :]).reshape(k, n).astype(np.float32)
    words = np.ascontiguousarray(scaled.reshape(k // 512, 128, 4, n).transpose(0, 1, 3, 2)).astype(ml_dtypes.float8_e4m3fn).view(np.uint8)
    return words, np.ascontiguousarray(byte.astype(np.uint8).reshape(k // 512, 16, n))


def unpack_weight(words, scales):
    g, p, n, _ = words.shape
    vals = np.ascontiguousarray(words).view(ml_dtypes.float8_e4m3fn).astype(np.float64) * np.repeat(np.exp2(scales.astype(np.float64) - 127.0), 8, axis=1)[..., None]
    return vals.transpose(0, 1, 3, 2).reshape(g * 512, n)


E2M1 = np.array([0.0, 0.5, 1.0, 1.5, 2.0, 3.0, 4.0, 6.0, -0.0, -0.5, -1.0, -1.5, -2.0, -3.0, -4.0, -6.0])


def pack_fp4(w):
    k, n = w.shape
    w = f64(np.asarray(w, np.float32).astype(ml_dtypes.bfloat16)).reshape(k // 32, 32, n)
    amax = np.abs(w).max(1)
    mant, ex = np.frexp(amax / 6.0)
    byte = np.clip(np.where(amax > 0, np.where(mant > 0.5, ex, ex - 1) + 127, 1), 1, 254)
    scaled = (w * np.exp2(127.0 - byte)[:, None, :]).reshape(k, n).astype(np.float32)
    c = np.ascontiguousarray(scaled.reshape(k // 512, 128, 4, n).transpose(0, 1, 3, 2)).astype(ml_dtypes.float4_e2m1fn).view(np.uint8) & 0xF
    words = (c[..., 0::2] | (c[..., 1::2] << 4)).reshape(k // 512, 128, 2 * n)
    return np.ascontiguousarray(words), np.ascontiguousarray(byte.astype(np.uint8).reshape(k // 512, 16, n))


def unpack_fp4(words, scales):
    g, _, n = scales.shape
    words = np.ascontiguousarray(words).reshape(g, 128, n, 2)
    nib = np.empty((g, 128, n, 4), np.uint8)
    nib[..., 0::2] = words & 0xF
    nib[..., 1::2] = words >> 4
    vals = E2M1[nib] * np.repeat(np.exp2(scales.astype(np.float64) - 127.0), 8, axis=1)[..., None]
    return vals.transpose(0, 1, 3, 2).reshape(g * 512, n)


def relu(v):
    return np.maximum(v, 0.0)


def sigmoid(v):
    return 1.0 / (1.0 + np.exp(-np.maximum(v, -700.0)))


K, T, S, N, H = 512, 2048, 512, 256, 512


def setup_inputs():
    n = np.random.standard_normal
    s = mx_kscale(K)[:, None]
    u = mx_kscale(H)
    packed_xT = pack_weight(n((K, T)) * s)
    packed_w1 = pack_fp4(n((K, H)) / np.sqrt(K) / s)
    packed_w2 = pack_fp4(n((H, N)) / np.sqrt(H) / u[:, None])
    return {
        "x_words": packed_xT[0],
        "x_scales": packed_xT[1],
        "w1_words": packed_w1[0],
        "w1_scales": packed_w1[1],
        "th1": (-np.random.uniform(0.1, 0.6, (H, 1))).astype(np.float32),
        "unit": (np.random.uniform(0.6, 1.4, (H, 1)) * u[:, None]).astype(np.float32),
        "w2_words": packed_w2[0],
        "w2_scales": packed_w2[1],
        "offs": striped(np.random.permutation(T)[:S]),
        "par": striped(np.random.permutation(S)),
    }


def reference(x_words, x_scales, w1_words, w1_scales, th1, unit, w2_words, w2_scales, offs, par):
    xq = unpack_weight(x_words, x_scales)[:, unstriped(offs)]
    y = unpack_fp4(w1_words, w1_scales).T @ xq
    ft = relu(y + f64(th1))
    fp = ft[:, unstriped(par)]
    child = ft * sigmoid(4.0 * fp - 1.0)
    both = child + fp
    hid = f64(unit) * (both - (0.7 * np.sqrt(ft * fp + 0.02)))
    return unpack_fp4(w2_words, w2_scales).T @ mxq(hid, 0, "e4m3")

@@ -1,0 +1,186 @@
+from contextlib import ExitStack
+
+import concourse.mybir as mybir
+
+K, T, S, N, H = 512, 2048, 512, 256, 512
+FLOPS = 2 * K * H * S + 2 * H * N * S
+
+F32 = mybir.dt.float32
+BF16 = mybir.dt.bfloat16
+I32 = mybir.dt.int32
+U32 = mybir.dt.uint32
+U16 = mybir.dt.uint16
+U8 = mybir.dt.uint8
+FP8X4 = mybir.dt.float8_e4m3fn_x4
+FP4X4 = mybir.dt.float4_e2m1fn_x4
+ALU = mybir.AluOpType
+ACT = mybir.ActivationFunctionType
+
+P = 128
+PACK = 4
+HALF = S // 2
+LIST_COLS = HALF // 16
+
+
+def tile_picked_ysaemt_root_p_kernel(tc, x_words, x_scales, w1_words, w1_scales, th1, unit, w2_words, w2_scales, offs, par, out):
+    nc = tc.nc
+    with ExitStack() as ctx:
+        lists = ctx.enter_context(tc.tile_pool(name="lists", bufs=1))
+        sb = ctx.enter_context(tc.tile_pool(name="sb", bufs=1))
+        ps = ctx.enter_context(tc.psum_pool(name="ps", bufs=1))
+
+        offs_sb = lists.tile([P, S // 16], U16, name="offs_sb")
+        par_sb = lists.tile([P, S // 16], U16, name="par_sb")
+        xw = sb.tile([P, T], U32, name="xw", align_bytes=64)
+        xs = sb.tile([P, T], U8, name="xs", tag="xs", align_bytes=64)
+        w1w = sb.tile([P, 2 * H], U8, name="w1w", align_bytes=64)
+        w1s = sb.tile([P, H], U8, name="w1s", align_bytes=64)
+        w2w = sb.tile([P, 2 * N], U8, name="w2w", align_bytes=64)
+        w2s = sb.tile([P, N], U8, name="w2s", align_bytes=64)
+        th_sb = sb.tile([P, PACK], F32, name="th_sb")
+        unit_sb = sb.tile([P, PACK], F32, name="unit_sb")
+        nu_sb = sb.tile([P, PACK], F32, name="nu_sb")
+
+        def load_scale_rows(eng, tile, rows, q):
+            eng.dma_start(tile[32 * q : 32 * q + 4, :].bitcast(I32), rows[0, 4 * q : 4 * q + 4, :].bitcast(I32))
+
+        nc.vector.memset(xs[:].bitcast(I32), 0)
+        nc.gpsimd.memset(w1s[:].bitcast(I32), 0)
+        nc.vector.memset(w2s[:].bitcast(I32), 0)
+
+        nc.sync.dma_start(offs_sb[:], offs)
+        nc.sync.dma_start(par_sb[:], par)
+        nc.sync.dma_start(w1w[:].bitcast(I32), w1_words[0].bitcast(I32))
+        nc.sync.dma_start(xw[:].bitcast(I32), x_words[0].rearrange("p n t -> p (n t)").bitcast(I32))
+        for q in range(4):
+            load_scale_rows(nc.scalar, xs, x_scales, q)
+        for q in range(4):
+            load_scale_rows(nc.sync if q < 3 else nc.gpsimd, w1s, w1_scales, q)
+        nc.gpsimd.dma_start(th_sb[:], th1.rearrange("(p t) o -> p (t o)", t=PACK))
+        nc.gpsimd.dma_start(unit_sb[:], unit.rearrange("(p t) o -> p (t o)", t=PACK))
+        nc.gpsimd.dma_start(w2w[:].bitcast(I32), w2_words[0].bitcast(I32))
+        for q in range(4):
+            load_scale_rows(nc.sync, w2s, w2_scales, q)
+        nc.gpsimd.tensor_scalar(nu_sb[:], unit_sb[:], -0.7, 0.0, ALU.mult, ALU.add)
+
+        w1wd = sb.tile([P, 2 * H], U8, name="w1wd", align_bytes=64)
+        w1sd = sb.tile([P, H], U8, name="w1sd", align_bytes=64)
+        xsg = sb.tile([P, S], U8, name="xsg", align_bytes=64)
+        nc.vector.tensor_copy(
+            w1wd[:].rearrange("p (t m b) -> p t m b", t=PACK, b=2),
+            w1w[:].rearrange("p (m t b) -> p t m b", t=PACK, b=2),
+        )
+        nc.vector.tensor_copy(xsg[:], xs[:].indirect(offs_sb[:]))
+        xg = [
+            sb.tile([P, HALF], U32, name="xg0", tag="xs", align_bytes=64),
+            sb.tile([P, HALF], U32, name="xg1", align_bytes=64),
+        ]
+        w1s_by_t = w1s[:].rearrange("p (m t) -> p t m", t=PACK)
+        w1sd_by_t = w1sd[:].rearrange("p (t m) -> p t m", t=PACK)
+        nc.vector.tensor_copy(w1sd_by_t[:, 0:1, :], w1s_by_t[:, 0:1, :])
+        for h in range(2):
+            nc.vector.tensor_copy(xg[h][:], xw[:].indirect(offs_sb[:, h * LIST_COLS : (h + 1) * LIST_COLS]))
+        nc.vector.tensor_copy(w1sd_by_t[:, 1:PACK, :], w1s_by_t[:, 1:PACK, :])
+
+        ft = [sb.tile([P, S], F32, name=f"ft{t}") for t in range(PACK)]
+        fp = [sb.tile([P, S], F32, name=f"fp{t}") for t in range(PACK)]
+        sg = [sb.tile([P, S], F32, name=f"sg{t}") for t in range(PACK)]
+        ch = [sb.tile([P, S], F32, name=f"ch{t}") for t in range(PACK)]
+        bo = [sb.tile([P, S], F32, name=f"bo{t}") for t in range(PACK)]
+        prod = sb.tile([P, PACK, S], F32, name="prod")
+        root = sb.tile([P, PACK, S], F32, name="root")
+
+        for t in range(PACK):
+            for h in range(2):
+                cols = slice(h * HALF, (h + 1) * HALF)
+                y = ps.tile([P, HALF], F32, name=f"y{t}{h}", tag=f"bank{t}{h}")
+                nc.tensor.matmul_mx(
+                    out=y[:],
+                    lhsT=w1wd[:, 2 * P * t : 2 * P * (t + 1)].bitcast(FP4X4),
+                    lhsT_scale=w1sd[:, P * t : P * (t + 1)],
+                    rhs=xg[h][:].bitcast(FP8X4),
+                    rhs_scale=xsg[:, cols],
+                    start=True,
+                    stop=True,
+                )
+                nc.scalar.activation(ft[t][:, cols], y[:], ACT.Relu, bias=th_sb[:, t : t + 1])
+
+        def gather(t, h, on_vector):
+            cols = slice(h * HALF, (h + 1) * HALF)
+            window = ft[t][:].indirect(par_sb[:, h * LIST_COLS : (h + 1) * LIST_COLS])
+            if on_vector:
+                nc.vector.tensor_copy(fp[t][:, cols], window)
+            else:
+                nc.scalar.activation(fp[t][:, cols], window, ACT.Copy)
+
+        def sigm(t):
+            nc.scalar.activation(sg[t][:], fp[t][:], ACT.Sigmoid, bias=-1.0, scale=4.0)
+
+        def product(t):
+            nc.vector.tensor_tensor(prod[:, t, :], ft[t][:], fp[t][:], ALU.mult)
+
+        def child(t):
+            nc.vector.scalar_tensor_tensor(ch[t][:], ft[t][:], unit_sb[:, t : t + 1], sg[t][:], ALU.mult, ALU.mult)
+
+        def both(t):
+            nc.vector.scalar_tensor_tensor(bo[t][:], fp[t][:], unit_sb[:, t : t + 1], ch[t][:], ALU.mult, ALU.add)
+
+        for t in range(PACK):
+            for h in range(2):
+                gather(t, h, t < 2)
+            if t == 2:
+                sigm(0)
+        for t in range(1, PACK):
+            sigm(t)
+        for t in range(3):
+            product(t)
+        child(0)
+        product(3)
+        child(1)
+        both(0)
+        both(1)
+        child(2)
+        child(3)
+        both(2)
+        both(3)
+
+        out_v = out.rearrange("(a p) j -> p a j", p=P)
+        for h in range(2):
+            cols = slice(h * HALF, (h + 1) * HALF)
+            for t in range(PACK):
+                nc.scalar.activation(root[:, t, cols], prod[:, t, cols], ACT.Sqrt, bias=0.02)
+        for h in range(2):
+            cols = slice(h * HALF, (h + 1) * HALF)
+            hb = sb.tile([P, PACK, HALF], BF16, name=f"hb{h}", align_bytes=64)
+            hi = sb.tile([P, HALF, PACK], BF16, name=f"hi{h}", align_bytes=64)
+            hq = sb.tile([P, HALF], U32, name=f"hq{h}", align_bytes=64)
+            hs = sb.tile([P, HALF], U8, name=f"hs{h}", align_bytes=64)
+            res = sb.tile([P, 2, HALF], F32, name=f"res{h}", align_bytes=64)
+            for t in range(PACK):
+                nc.vector.scalar_tensor_tensor(hb[:, t, :], root[:, t, cols], nu_sb[:, t : t + 1], bo[t][:, cols], ALU.mult, ALU.add)
+            dst = hi[:].rearrange("p (c i) t -> p c t i", i=4)
+            src = hb[:].rearrange("p t (c i) -> p c t i", i=4)
+            if h == 0:
+                nc.scalar.copy(dst, src)
+            else:
+                nc.vector.tensor_copy(dst, src)
+            nc.vector.quantize_mx(out=hq[:].bitcast(FP8X4), scales=hs[:], in_=hi[:].rearrange("p c t -> p (c t)"))
+            for a in range(2):
+                acc = ps.tile([P, HALF], F32, name=f"acc{h}{a}", tag=f"bank{h}{a}")
+                nc.tensor.matmul_mx(
+                    out=acc[:],
+                    lhsT=w2w[:, 2 * P * a : 2 * P * (a + 1)].bitcast(FP4X4),
+                    lhsT_scale=w2s[:, P * a : P * (a + 1)],
+                    rhs=hq[:].bitcast(FP8X4),
+                    rhs_scale=hs[:],
+                    start=True,
+                    stop=True,
+                )
+                if h == 1 and a == 1:
+                    nc.vector.tensor_copy(res[:, a, :], acc[:])
+                else:
+                    nc.scalar.copy(res[:, a, :], acc[:])
+                if h == 1:
+                    (nc.scalar if a == 0 else nc.sync).dma_start(out_v[:, a, cols], res[:, a, :])
+            if h == 0:
+                nc.sync.dma_start(out_v[:, :, cols], res[:])

@@ -31,37 +31,33 @@ def tile_picked_ysaemt_root_p_kernel(tc, x_words, x_scales, w1_words, w1_scales,
 
         offs_sb = lists.tile([P, S // 16], U16, name="offs_sb")
         par_sb = lists.tile([P, S // 16], U16, name="par_sb")
-        xw = sb.tile([P, T], U32, name="xw", align_bytes=64)
+        ones = sb.tile([P, 1], F32, name="ones", tag="xw", align_bytes=64)
+        root_bias = sb.tile([P, 1], F32, name="root_bias")
         xs = sb.tile([P, T], U8, name="xs", tag="xs", align_bytes=64)
-        w1w = sb.tile([P, 2 * H], U8, name="w1w", align_bytes=64)
-        w1s = sb.tile([P, H], U8, name="w1s", align_bytes=64)
-        w2w = sb.tile([P, 2 * N], U8, name="w2w", align_bytes=64)
-        w2s = sb.tile([P, N], U8, name="w2s", align_bytes=64)
-        th_sb = sb.tile([P, PACK], F32, name="th_sb")
-        unit_sb = sb.tile([P, PACK], F32, name="unit_sb")
-        nu_sb = sb.tile([P, PACK], F32, name="nu_sb")
+        w1w = sb.tile([P, 2 * H], U8, name="w1w", tag="w1w", align_bytes=64)
+        w1s = sb.tile([P, H], U8, name="w1s", tag="w1s", align_bytes=64)
 
         def load_scale_rows(eng, tile, rows, q):
             eng.dma_start(tile[32 * q : 32 * q + 4, :].bitcast(I32), rows[0, 4 * q : 4 * q + 4, :].bitcast(I32))
 
         nc.vector.memset(xs[:].bitcast(I32), 0)
-        nc.gpsimd.memset(w1s[:].bitcast(I32), 0)
-        nc.vector.memset(w2s[:].bitcast(I32), 0)
+        nc.vector.memset(ones[:], 1.0)
+        nc.vector.tensor_scalar(root_bias[:], ones[:], 0.02, None, ALU.mult)
+        nc.vector.memset(w1s[:].bitcast(I32), 0)
+        xw = sb.tile([P, T], U32, name="xw", tag="xw", align_bytes=64)
 
         nc.sync.dma_start(offs_sb[:], offs)
         nc.sync.dma_start(par_sb[:], par)
         nc.sync.dma_start(w1w[:].bitcast(I32), w1_words[0].bitcast(I32))
+        for q in range(4):
+            load_scale_rows(nc.sync, xs, x_scales, q)
         nc.sync.dma_start(xw[:].bitcast(I32), x_words[0].rearrange("p n t -> p (n t)").bitcast(I32))
         for q in range(4):
-            load_scale_rows(nc.scalar, xs, x_scales, q)
-        for q in range(4):
-            load_scale_rows(nc.sync if q < 3 else nc.gpsimd, w1s, w1_scales, q)
-        nc.gpsimd.dma_start(th_sb[:], th1.rearrange("(p t) o -> p (t o)", t=PACK))
-        nc.gpsimd.dma_start(unit_sb[:], unit.rearrange("(p t) o -> p (t o)", t=PACK))
-        nc.gpsimd.dma_start(w2w[:].bitcast(I32), w2_words[0].bitcast(I32))
-        for q in range(4):
-            load_scale_rows(nc.sync, w2s, w2_scales, q)
-        nc.gpsimd.tensor_scalar(nu_sb[:], unit_sb[:], -0.7, 0.0, ALU.mult, ALU.add)
+            load_scale_rows(nc.sync, w1s, w1_scales, q)
+        warm_in = sb.tile([P, 1], F32, name="warm_in")
+        warm_out = sb.tile([P, 1], F32, name="warm_out")
+        nc.vector.memset(warm_in[:], 0.0)
+        nc.scalar.activation(warm_out[:], warm_in[:], ACT.Sigmoid, bias=-1.0, scale=4.0)
 
         w1wd = sb.tile([P, 2 * H], U8, name="w1wd", align_bytes=64)
         w1sd = sb.tile([P, H], U8, name="w1sd", align_bytes=64)
@@ -70,25 +66,33 @@ def tile_picked_ysaemt_root_p_kernel(tc, x_words, x_scales, w1_words, w1_scales,
             w1wd[:].rearrange("p (t m b) -> p t m b", t=PACK, b=2),
             w1w[:].rearrange("p (m t b) -> p t m b", t=PACK, b=2),
         )
+        th_sb = sb.tile([P, PACK], F32, name="th_sb", tag="w1w", align_bytes=64)
+        nc.sync.dma_start(th_sb[:], th1.rearrange("(p t) o -> p (t o)", t=PACK))
         nc.vector.tensor_copy(xsg[:], xs[:].indirect(offs_sb[:]))
         xg = [
             sb.tile([P, HALF], U32, name="xg0", tag="xs", align_bytes=64),
-            sb.tile([P, HALF], U32, name="xg1", align_bytes=64),
+            sb.tile([P, HALF], U32, name="xg1", tag="sg0", align_bytes=64),
         ]
         w1s_by_t = w1s[:].rearrange("p (m t) -> p t m", t=PACK)
         w1sd_by_t = w1sd[:].rearrange("p (t m) -> p t m", t=PACK)
-        nc.vector.tensor_copy(w1sd_by_t[:, 0:1, :], w1s_by_t[:, 0:1, :])
         for h in range(2):
             nc.vector.tensor_copy(xg[h][:], xw[:].indirect(offs_sb[:, h * LIST_COLS : (h + 1) * LIST_COLS]))
-        nc.vector.tensor_copy(w1sd_by_t[:, 1:PACK, :], w1s_by_t[:, 1:PACK, :])
+            planes = slice(0, 1) if h == 0 else slice(1, PACK)
+            nc.vector.tensor_copy(w1sd_by_t[:, planes, :], w1s_by_t[:, planes, :])
 
-        ft = [sb.tile([P, S], F32, name=f"ft{t}") for t in range(PACK)]
+        unit_sb = sb.tile([P, PACK], F32, name="unit_sb", tag="w1s", align_bytes=64)
+        nu_sb = sb.tile([P, PACK], F32, name="nu_sb")
+        w2w = sb.tile([P, 2 * N], U8, name="w2w", tag="xw", align_bytes=64)
+        w2s = sb.tile([P, N], U8, name="w2s", tag="xs", align_bytes=64)
+        nc.sync.dma_start(unit_sb[:], unit.rearrange("(p t) o -> p (t o)", t=PACK))
+        nc.sync.dma_start(w2w[:].bitcast(I32), w2_words[0].bitcast(I32))
+
+        ft = [sb.tile([P, S], F32, name=f"ft{t}", tag=f"ft{t}") for t in range(PACK)]
         fp = [sb.tile([P, S], F32, name=f"fp{t}") for t in range(PACK)]
-        sg = [sb.tile([P, S], F32, name=f"sg{t}") for t in range(PACK)]
+        sg = [sb.tile([P, S], F32, name=f"sg{t}", tag=f"sg{t}", align_bytes=64) for t in range(PACK)]
         ch = [sb.tile([P, S], F32, name=f"ch{t}") for t in range(PACK)]
-        bo = [sb.tile([P, S], F32, name=f"bo{t}") for t in range(PACK)]
+        bo = {}
         prod = sb.tile([P, PACK, S], F32, name="prod")
-        root = sb.tile([P, PACK, S], F32, name="root")
 
         for t in range(PACK):
             for h in range(2):
@@ -123,32 +127,42 @@ def tile_picked_ysaemt_root_p_kernel(tc, x_words, x_scales, w1_words, w1_scales,
             nc.vector.scalar_tensor_tensor(ch[t][:], ft[t][:], unit_sb[:, t : t + 1], sg[t][:], ALU.mult, ALU.mult)
 
         def both(t):
+            bo[t] = sb.tile([P, S], F32, name=f"bo{t}", tag=f"sg{t ^ 1}", align_bytes=64)
             nc.vector.scalar_tensor_tensor(bo[t][:], fp[t][:], unit_sb[:, t : t + 1], ch[t][:], ALU.mult, ALU.add)
 
-        for t in range(PACK):
-            for h in range(2):
-                gather(t, h, t < 2)
-            if t == 2:
-                sigm(0)
-        for t in range(1, PACK):
+        gather(0, 0, True)
+        gather(0, 1, True)
+        gather(1, 0, True)
+        gather(1, 1, False)
+        for t in range(2):
             sigm(t)
-        for t in range(3):
-            product(t)
+            gather(t + 2, 0, False)
+            gather(t + 2, 1, False)
+        sigm(2)
+        sigm(3)
+        product(0)
+        product(1)
         child(0)
-        product(3)
+        product(2)
         child(1)
+        product(3)
         both(0)
         both(1)
         child(2)
         child(3)
         both(2)
         both(3)
+        nc.vector.memset(w2s[:].bitcast(I32), 0)
+        for q in range(4):
+            load_scale_rows(nc.sync, w2s, w2_scales, q)
+        nc.vector.tensor_scalar(nu_sb[:], unit_sb[:], -0.7, None, ALU.mult)
 
+        root = [sb.tile([P, 2, S], F32, name="root01", tag="ft3"), sb.tile([P, 2, S], F32, name="root23")]
         out_v = out.rearrange("(a p) j -> p a j", p=P)
         for h in range(2):
             cols = slice(h * HALF, (h + 1) * HALF)
-            for t in range(PACK):
-                nc.scalar.activation(root[:, t, cols], prod[:, t, cols], ACT.Sqrt, bias=0.02)
+            for pair in (1, 0):
+                nc.scalar.activation(root[pair][:, :, cols], prod[:, 2 * pair : 2 * pair + 2, cols], ACT.Sqrt, bias=root_bias[:])
         for h in range(2):
             cols = slice(h * HALF, (h + 1) * HALF)
             hb = sb.tile([P, PACK, HALF], BF16, name=f"hb{h}", align_bytes=64)
@@ -156,8 +170,8 @@ def tile_picked_ysaemt_root_p_kernel(tc, x_words, x_scales, w1_words, w1_scales,
             hq = sb.tile([P, HALF], U32, name=f"hq{h}", align_bytes=64)
             hs = sb.tile([P, HALF], U8, name=f"hs{h}", align_bytes=64)
             res = sb.tile([P, 2, HALF], F32, name=f"res{h}", align_bytes=64)
-            for t in range(PACK):
-                nc.vector.scalar_tensor_tensor(hb[:, t, :], root[:, t, cols], nu_sb[:, t : t + 1], bo[t][:, cols], ALU.mult, ALU.add)
+            for t in (2, 3, 0, 1):
+                nc.vector.scalar_tensor_tensor(hb[:, t, :], root[t // 2][:, t % 2, cols], nu_sb[:, t : t + 1], bo[t][:, cols], ALU.mult, ALU.add)
             dst = hi[:].rearrange("p (c i) t -> p c t i", i=4)
             src = hb[:].rearrange("p t (c i) -> p c t i", i=4)
             if h == 0:

@@ -66,8 +66,11 @@ def tile_picked_ysaemt_root_p_kernel(tc, x_words, x_scales, w1_words, w1_scales,
             w1wd[:].rearrange("p (t m b) -> p t m b", t=PACK, b=2),
             w1w[:].rearrange("p (m t b) -> p t m b", t=PACK, b=2),
         )
-        th_sb = sb.tile([P, PACK], F32, name="th_sb", tag="w1w", align_bytes=64)
-        nc.sync.dma_start(th_sb[:], th1.rearrange("(p t) o -> p (t o)", t=PACK))
+        rowc = sb.tile([P, 16], F32, name="rowc", tag="w1w", align_bytes=64)
+        th_sb = rowc[:, 0:PACK]
+        unit_sb = rowc[:, 8 : 8 + PACK]
+        nc.sync.dma_start(th_sb, th1.rearrange("(p t) o -> p (t o)", t=PACK))
+        nc.sync.dma_start(unit_sb, unit.rearrange("(p t) o -> p (t o)", t=PACK))
         nc.vector.tensor_copy(xsg[:], xs[:].indirect(offs_sb[:]))
         xg = [
             sb.tile([P, HALF], U32, name="xg0", tag="xs", align_bytes=64),
@@ -80,11 +83,10 @@ def tile_picked_ysaemt_root_p_kernel(tc, x_words, x_scales, w1_words, w1_scales,
             planes = slice(0, 1) if h == 0 else slice(1, PACK)
             nc.vector.tensor_copy(w1sd_by_t[:, planes, :], w1s_by_t[:, planes, :])
 
-        unit_sb = sb.tile([P, PACK], F32, name="unit_sb", tag="w1s", align_bytes=64)
         nu_sb = sb.tile([P, PACK], F32, name="nu_sb")
         w2w = sb.tile([P, 2 * N], U8, name="w2w", tag="xw", align_bytes=64)
         w2s = sb.tile([P, N], U8, name="w2s", tag="xs", align_bytes=64)
-        nc.sync.dma_start(unit_sb[:], unit.rearrange("(p t) o -> p (t o)", t=PACK))
+        nc.vector.tensor_scalar(nu_sb[:], unit_sb, -0.7, None, ALU.mult)
         nc.sync.dma_start(w2w[:].bitcast(I32), w2_words[0].bitcast(I32))
 
         ft = [sb.tile([P, S], F32, name=f"ft{t}", tag=f"ft{t}") for t in range(PACK)]
@@ -133,7 +135,7 @@ def tile_picked_ysaemt_root_p_kernel(tc, x_words, x_scales, w1_words, w1_scales,
         gather(0, 0, True)
         gather(0, 1, True)
         gather(1, 0, True)
-        gather(1, 1, False)
+        gather(1, 1, True)
         for t in range(2):
             sigm(t)
             gather(t + 2, 0, False)
@@ -152,10 +154,9 @@ def tile_picked_ysaemt_root_p_kernel(tc, x_words, x_scales, w1_words, w1_scales,
         child(3)
         both(2)
         both(3)
-        nc.vector.memset(w2s[:].bitcast(I32), 0)
+        nc.gpsimd.memset(w2s[:].bitcast(I32), 0)
         for q in range(4):
             load_scale_rows(nc.sync, w2s, w2_scales, q)
-        nc.vector.tensor_scalar(nu_sb[:], unit_sb[:], -0.7, None, ALU.mult)
 
         root = [sb.tile([P, 2, S], F32, name="root01", tag="ft3"), sb.tile([P, 2, S], F32, name="root23")]
         out_v = out.rearrange("(a p) j -> p a j", p=P)
@@ -177,7 +178,8 @@ def tile_picked_ysaemt_root_p_kernel(tc, x_words, x_scales, w1_words, w1_scales,
             if h == 0:
                 nc.scalar.copy(dst, src)
             else:
-                nc.vector.tensor_copy(dst, src)
+                nc.vector.tensor_copy(dst[:, :40], src[:, :40])
+                nc.scalar.copy(dst[:, 40:], src[:, 40:])
             nc.vector.quantize_mx(out=hq[:].bitcast(FP8X4), scales=hs[:], in_=hi[:].rearrange("p c t -> p (c t)"))
             for a in range(2):
                 acc = ps.tile([P, HALF], F32, name=f"acc{h}{a}", tag=f"bank{h}{a}")

from contextlib import ExitStack

import concourse.mybir as mybir

K, T, S, N, H = 512, 2048, 512, 256, 512
FLOPS = 2 * K * H * S + 2 * H * N * S

F32 = mybir.dt.float32
BF16 = mybir.dt.bfloat16
I32 = mybir.dt.int32
U32 = mybir.dt.uint32
U16 = mybir.dt.uint16
U8 = mybir.dt.uint8
FP8X4 = mybir.dt.float8_e4m3fn_x4
FP4X4 = mybir.dt.float4_e2m1fn_x4
ALU = mybir.AluOpType
ACT = mybir.ActivationFunctionType

P = 128
PACK = 4
HALF = S // 2
LIST_COLS = HALF // 16


def tile_picked_ysaemt_root_p_kernel(tc, x_words, x_scales, w1_words, w1_scales, th1, unit, w2_words, w2_scales, offs, par, out):
    nc = tc.nc
    with ExitStack() as ctx:
        lists = ctx.enter_context(tc.tile_pool(name="lists", bufs=1))
        sb = ctx.enter_context(tc.tile_pool(name="sb", bufs=1))
        ps = ctx.enter_context(tc.psum_pool(name="ps", bufs=1))

        offs_sb = lists.tile([P, S // 16], U16, name="offs_sb")
        par_sb = lists.tile([P, S // 16], U16, name="par_sb")
        ones = sb.tile([P, 1], F32, name="ones", tag="xw", align_bytes=64)
        root_bias = sb.tile([P, 1], F32, name="root_bias")
        xs = sb.tile([P, T], U8, name="xs", tag="xs", align_bytes=64)
        w1w = sb.tile([P, 2 * H], U8, name="w1w", tag="w1w", align_bytes=64)
        w1s = sb.tile([P, H], U8, name="w1s", tag="w1s", align_bytes=64)

        def load_scale_rows(eng, tile, rows, q):
            eng.dma_start(tile[32 * q : 32 * q + 4, :].bitcast(I32), rows[0, 4 * q : 4 * q + 4, :].bitcast(I32))

        nc.vector.memset(xs[:].bitcast(I32), 0)
        nc.vector.memset(ones[:], 1.0)
        nc.vector.tensor_scalar(root_bias[:], ones[:], 0.02, None, ALU.mult)
        nc.vector.memset(w1s[:].bitcast(I32), 0)
        xw = sb.tile([P, T], U32, name="xw", tag="xw", align_bytes=64)

        nc.sync.dma_start(offs_sb[:], offs)
        nc.sync.dma_start(par_sb[:], par)
        nc.sync.dma_start(w1w[:].bitcast(I32), w1_words[0].bitcast(I32))
        for q in range(4):
            load_scale_rows(nc.sync, xs, x_scales, q)
        nc.sync.dma_start(xw[:].bitcast(I32), x_words[0].rearrange("p n t -> p (n t)").bitcast(I32))
        for q in range(4):
            load_scale_rows(nc.sync, w1s, w1_scales, q)
        warm_in = sb.tile([P, 1], F32, name="warm_in")
        warm_out = sb.tile([P, 1], F32, name="warm_out")
        nc.vector.memset(warm_in[:], 0.0)
        nc.scalar.activation(warm_out[:], warm_in[:], ACT.Sigmoid, bias=-1.0, scale=4.0)

        w1wd = sb.tile([P, 2 * H], U8, name="w1wd", align_bytes=64)
        w1sd = sb.tile([P, H], U8, name="w1sd", align_bytes=64)
        xsg = sb.tile([P, S], U8, name="xsg", align_bytes=64)
        nc.vector.tensor_copy(
            w1wd[:].rearrange("p (t m b) -> p t m b", t=PACK, b=2),
            w1w[:].rearrange("p (m t b) -> p t m b", t=PACK, b=2),
        )
        rowc = sb.tile([P, 16], F32, name="rowc", tag="w1w", align_bytes=64)
        th_sb = rowc[:, 0:PACK]
        unit_sb = rowc[:, 8 : 8 + PACK]
        nc.sync.dma_start(th_sb, th1.rearrange("(p t) o -> p (t o)", t=PACK))
        nc.sync.dma_start(unit_sb, unit.rearrange("(p t) o -> p (t o)", t=PACK))
        nc.vector.tensor_copy(xsg[:], xs[:].indirect(offs_sb[:]))
        xg = [
            sb.tile([P, HALF], U32, name="xg0", tag="xs", align_bytes=64),
            sb.tile([P, HALF], U32, name="xg1", tag="sg0", align_bytes=64),
        ]
        w1s_by_t = w1s[:].rearrange("p (m t) -> p t m", t=PACK)
        w1sd_by_t = w1sd[:].rearrange("p (t m) -> p t m", t=PACK)
        for h in range(2):
            nc.vector.tensor_copy(xg[h][:], xw[:].indirect(offs_sb[:, h * LIST_COLS : (h + 1) * LIST_COLS]))
            planes = slice(0, 1) if h == 0 else slice(1, PACK)
            nc.vector.tensor_copy(w1sd_by_t[:, planes, :], w1s_by_t[:, planes, :])

        nu_sb = sb.tile([P, PACK], F32, name="nu_sb")
        w2w = sb.tile([P, 2 * N], U8, name="w2w", tag="xw", align_bytes=64)
        w2s = sb.tile([P, N], U8, name="w2s", tag="xs", align_bytes=64)
        nc.vector.tensor_scalar(nu_sb[:], unit_sb, -0.7, None, ALU.mult)
        nc.sync.dma_start(w2w[:].bitcast(I32), w2_words[0].bitcast(I32))

        ft = [sb.tile([P, S], F32, name=f"ft{t}", tag=f"ft{t}") for t in range(PACK)]
        fp = [sb.tile([P, S], F32, name=f"fp{t}") for t in range(PACK)]
        sg = [sb.tile([P, S], F32, name=f"sg{t}", tag=f"sg{t}", align_bytes=64) for t in range(PACK)]
        ch = [sb.tile([P, S], F32, name=f"ch{t}") for t in range(PACK)]
        bo = {}
        prod = sb.tile([P, PACK, S], F32, name="prod")

        for t in range(PACK):
            for h in range(2):
                cols = slice(h * HALF, (h + 1) * HALF)
                y = ps.tile([P, HALF], F32, name=f"y{t}{h}", tag=f"bank{t}{h}")
                nc.tensor.matmul_mx(
                    out=y[:],
                    lhsT=w1wd[:, 2 * P * t : 2 * P * (t + 1)].bitcast(FP4X4),
                    lhsT_scale=w1sd[:, P * t : P * (t + 1)],
                    rhs=xg[h][:].bitcast(FP8X4),
                    rhs_scale=xsg[:, cols],
                    start=True,
                    stop=True,
                )
                nc.scalar.activation(ft[t][:, cols], y[:], ACT.Relu, bias=th_sb[:, t : t + 1])

        def gather(t, h, on_vector):
            cols = slice(h * HALF, (h + 1) * HALF)
            window = ft[t][:].indirect(par_sb[:, h * LIST_COLS : (h + 1) * LIST_COLS])
            if on_vector:
                nc.vector.tensor_copy(fp[t][:, cols], window)
            else:
                nc.scalar.activation(fp[t][:, cols], window, ACT.Copy)

        def sigm(t):
            nc.scalar.activation(sg[t][:], fp[t][:], ACT.Sigmoid, bias=-1.0, scale=4.0)

        def product(t):
            nc.vector.tensor_tensor(prod[:, t, :], ft[t][:], fp[t][:], ALU.mult)

        def child(t):
            nc.vector.scalar_tensor_tensor(ch[t][:], ft[t][:], unit_sb[:, t : t + 1], sg[t][:], ALU.mult, ALU.mult)

        def both(t):
            bo[t] = sb.tile([P, S], F32, name=f"bo{t}", tag=f"sg{t ^ 1}", align_bytes=64)
            nc.vector.scalar_tensor_tensor(bo[t][:], fp[t][:], unit_sb[:, t : t + 1], ch[t][:], ALU.mult, ALU.add)

        gather(0, 0, True)
        gather(0, 1, True)
        gather(1, 0, True)
        gather(1, 1, True)
        for t in range(2):
            sigm(t)
            gather(t + 2, 0, False)
            gather(t + 2, 1, False)
        sigm(2)
        sigm(3)
        product(0)
        product(1)
        child(0)
        product(2)
        child(1)
        product(3)
        both(0)
        both(1)
        child(2)
        child(3)
        both(2)
        both(3)
        nc.gpsimd.memset(w2s[:].bitcast(I32), 0)
        for q in range(4):
            load_scale_rows(nc.sync, w2s, w2_scales, q)

        root = [sb.tile([P, 2, S], F32, name="root01", tag="ft3"), sb.tile([P, 2, S], F32, name="root23")]
        out_v = out.rearrange("(a p) j -> p a j", p=P)
        for h in range(2):
            cols = slice(h * HALF, (h + 1) * HALF)
            for pair in (1, 0):
                nc.scalar.activation(root[pair][:, :, cols], prod[:, 2 * pair : 2 * pair + 2, cols], ACT.Sqrt, bias=root_bias[:])
        for h in range(2):
            cols = slice(h * HALF, (h + 1) * HALF)
            hb = sb.tile([P, PACK, HALF], BF16, name=f"hb{h}", align_bytes=64)
            hi = sb.tile([P, HALF, PACK], BF16, name=f"hi{h}", align_bytes=64)
            hq = sb.tile([P, HALF], U32, name=f"hq{h}", align_bytes=64)
            hs = sb.tile([P, HALF], U8, name=f"hs{h}", align_bytes=64)
            res = sb.tile([P, 2, HALF], F32, name=f"res{h}", align_bytes=64)
            for t in (2, 3, 0, 1):
                nc.vector.scalar_tensor_tensor(hb[:, t, :], root[t // 2][:, t % 2, cols], nu_sb[:, t : t + 1], bo[t][:, cols], ALU.mult, ALU.add)
            dst = hi[:].rearrange("p (c i) t -> p c t i", i=4)
            src = hb[:].rearrange("p t (c i) -> p c t i", i=4)
            if h == 0:
                nc.scalar.copy(dst, src)
            else:
                nc.vector.tensor_copy(dst[:, :40], src[:, :40])
                nc.scalar.copy(dst[:, 40:], src[:, 40:])
            nc.vector.quantize_mx(out=hq[:].bitcast(FP8X4), scales=hs[:], in_=hi[:].rearrange("p c t -> p (c t)"))
            for a in range(2):
                acc = ps.tile([P, HALF], F32, name=f"acc{h}{a}", tag=f"bank{h}{a}")
                nc.tensor.matmul_mx(
                    out=acc[:],
                    lhsT=w2w[:, 2 * P * a : 2 * P * (a + 1)].bitcast(FP4X4),
                    lhsT_scale=w2s[:, P * a : P * (a + 1)],
                    rhs=hq[:].bitcast(FP8X4),
                    rhs_scale=hs[:],
                    start=True,
                    stop=True,
                )
                if h == 1 and a == 1:
                    nc.vector.tensor_copy(res[:, a, :], acc[:])
                else:
                    nc.scalar.copy(res[:, a, :], acc[:])
                if h == 1:
                    (nc.scalar if a == 0 else nc.sync).dma_start(out_v[:, a, cols], res[:, a, :])
            if h == 0:
                nc.sync.dma_start(out_v[:, :, cols], res[:])
